import numpy as np
import ml_dtypes


def mxq(x, axis, fmt="e4m3"):
    dtype, down = {"e4m3": (ml_dtypes.float8_e4m3fn, 7), "e5m2": (ml_dtypes.float8_e5m2, 14)}[fmt]
    v = np.moveaxis(np.asarray(x, np.float32).astype(ml_dtypes.bfloat16).astype(np.float64), axis, -1)
    blocks = v.reshape(v.shape[:-1] + (-1, 32))
    amax = np.abs(blocks).max(-1, keepdims=True)
    byte = np.maximum(np.where(amax > 0, np.frexp(amax)[1] - 1 + 127, 0) - down, 1)
    scale = np.exp2(byte - 127.0)
    codes = (blocks / scale).astype(np.float32).astype(dtype).astype(np.float64)
    return np.moveaxis((codes * scale).reshape(v.shape), -1, axis)


WIDE = False


def mx_kscale(k):
    if not WIDE:
        return np.ones(k)
    levels = np.array([10, -10, 5, -5, 0])
    if k % 512:
        return np.exp2(np.random.permutation(np.resize(levels, k // 32))).repeat(32)
    a = np.empty((k // 512, 16))
    for p in range(k // 512):
        a[p, :8] = np.random.permutation(np.resize(levels, 8))
        for g in range(8):
            far = levels[np.abs(levels - a[p, g]) >= 10]
            a[p, g + 8] = far[np.random.randint(len(far))]
    return np.exp2(a.ravel()).repeat(32)


def f64(x):
    return np.asarray(x).astype(np.float64)


def striped(idx):
    return np.tile(np.asarray(idx).reshape(-1, 16).T, (8, 1)).astype(np.uint16)


def unstriped(offs):
    return offs[:16].T.reshape(-1).astype(np.int64)


E2M1 = np.array([0.0, 0.5, 1.0, 1.5, 2.0, 3.0, 4.0, 6.0, -0.0, -0.5, -1.0, -1.5, -2.0, -3.0, -4.0, -6.0])


def pack_weight(w, fmt):
    k, n = w.shape
    w = f64(np.asarray(w, np.float32).astype(ml_dtypes.bfloat16)).reshape(k // 32, 32, n)
    amax = np.abs(w).max(1)
    if fmt == "e4m3":
        byte = np.frexp(amax)[1] - 1 + 127 - 7
    else:
        mant, ex = np.frexp(amax / 6.0)
        byte = np.where(mant > 0.5, ex, ex - 1) + 127
    byte = np.clip(np.where(amax > 0, byte, 1), 1, 254)
    scaled = (w * np.exp2(127.0 - byte)[:, None, :]).reshape(k, n).astype(np.float32)
    by_word = np.ascontiguousarray(scaled.reshape(k // 512, 128, 4, n).transpose(0, 1, 3, 2))
    if fmt == "e4m3":
        words = by_word.astype(ml_dtypes.float8_e4m3fn).view(np.uint8)
    else:
        c = by_word.astype(ml_dtypes.float4_e2m1fn).view(np.uint8) & 0xF
        words = (c[..., 0::2] | (c[..., 1::2] << 4)).reshape(k // 512, 128, 2 * n)
    return np.ascontiguousarray(words), np.ascontiguousarray(byte.astype(np.uint8).reshape(k // 512, 16, n))


def unpack_weight(words, scales, fmt):
    g, _, n = scales.shape
    words = np.ascontiguousarray(words).reshape(g, 128, n, -1)
    if fmt == "e4m3":
        vals = words.view(ml_dtypes.float8_e4m3fn).astype(np.float64)
    else:
        nib = np.empty((g, 128, n, 4), np.uint8)
        nib[..., 0::2] = words & 0xF
        nib[..., 1::2] = words >> 4
        vals = E2M1[nib]
    vals = vals * np.repeat(np.exp2(scales.astype(np.float64) - 127.0), 8, axis=1)[..., None]
    return vals.transpose(0, 1, 3, 2).reshape(g * 512, n)


D, T, I, Q, E = 512, 2048, 512, 128, 512


def setup_inputs():
    n = np.random.standard_normal
    idx = np.random.permutation(T)[:I]
    idx2 = np.random.randint(0, I, I)
    idx3 = np.random.randint(0, I, I)
    fd = mx_kscale(D)
    fi = mx_kscale(I)
    ti = np.ones(T)
    ti[idx] = fi
    keysp = pack_weight(n((D, T)) / fd[:, None], "e4m3")
    return {
        "query": (n((D, Q)) * 0.25 / np.sqrt(D) * fd[:, None]).astype(np.float32),
        "keys_words": keysp[0],
        "keys_scales": keysp[1],
        "sa": (np.random.uniform(0.3, 0.9, (1, I))).astype(np.float32),
        "sb": (np.random.uniform(-0.7, 0.7, (1, I))).astype(np.float32),
        "size": (np.random.uniform(0.5, 2.0, (1, I)) * fi).astype(np.float32),
        "vals": (n((E, T)) / ti).astype(np.float32),
        "offs": striped(idx),
        "offs2": striped(idx2),
        "offs3": striped(idx3),
    }


def reference(query, keys_words, keys_scales, sa, sb, size, vals, offs, offs2, offs3):
    idx = unstriped(offs)
    idx2 = unstriped(offs2)
    idx3 = unstriped(offs3)
    keysu = unpack_weight(keys_words, keys_scales, "e4m3")
    queryq = mxq(f64(query), 0, "e4m3")
    keysidxg = keysu[:, idx]
    a = queryq.T @ keysidxg
    s = a + a[:, idx2] * f64(sa) + a[:, idx3] * f64(sb)
    p = np.exp(s - np.max(s, axis=1, keepdims=True))
    w = p * f64(size) / np.sum(p, axis=1, keepdims=True)
    wt = w.T
    vt = f64(vals)[:, idx].T
    wtq = mxq(wt, 0, "e4m3")
    vtq = mxq(vt, 0, "e4m3")
    o = wtq.T @ vtq
    return o

@@ -1,0 +1,176 @@
+from contextlib import ExitStack
+
+import concourse.mybir as mybir
+from concourse.masks import make_identity
+
+D, T, I, Q, E = 512, 2048, 512, 128, 512
+FLOPS = 2 * D * Q * I + 2 * I * Q * E
+
+F32 = mybir.dt.float32
+BF16 = mybir.dt.bfloat16
+I32 = mybir.dt.int32
+U32 = mybir.dt.uint32
+U16 = mybir.dt.uint16
+U8 = mybir.dt.uint8
+FP8X4 = mybir.dt.float8_e4m3fn_x4
+ALU = mybir.AluOpType
+ACT = mybir.ActivationFunctionType
+AXIS = mybir.AxisListType
+
+P = 128
+PACK = 4
+BLOCKS = I // P
+HALF = I // 2
+LIST_COLS = I // 16
+
+
+def tile_attend_neighbourscores_kernel(tc, query, keys_words, keys_scales, sa, sb, size, vals, offs, offs2, offs3, out):
+    nc = tc.nc
+    with ExitStack() as ctx:
+        lists = ctx.enter_context(tc.tile_pool(name="lists", bufs=1))
+        sb_pool = ctx.enter_context(tc.tile_pool(name="work", bufs=1))
+        psum = ctx.enter_context(tc.psum_pool(name="psum", bufs=1))
+
+        def sbuf(name, shape, dtype):
+            return sb_pool.tile(shape, dtype, name=name, align_bytes=64)
+
+        def bank(tag, shape):
+            return psum.tile(shape, F32, name=tag, tag=tag)
+
+        def half_list(tile, h):
+            return tile[:, h * LIST_COLS // 2 : (h + 1) * LIST_COLS // 2]
+
+        key_list = lists.tile([P, LIST_COLS], U16, name="key_list")
+        link_lists = [lists.tile([P, LIST_COLS], U16, name=f"link_list{l}") for l in range(2)]
+        key_scales = sbuf("key_scales", [P, T], U8)
+        key_words = sbuf("key_words", [P, T], U32)
+        q_raw = sbuf("q_raw", [P, PACK, Q], F32)
+        rows = sbuf("rows", [P, P], F32)
+        pools = [sbuf(f"val_pool{j}", [P, T], F32) for j in range(E // P)]
+
+        nc.vector.memset(key_scales[:].bitcast(I32), 0)
+        nc.vector.memset(rows[:], 0.0)
+        nc.sync.dma_start(key_list[:], offs)
+        for g in range(4):
+            nc.sync.dma_start(key_scales[32 * g : 32 * g + 4, :].bitcast(I32), keys_scales[0, 4 * g : 4 * g + 4, :].bitcast(I32))
+        nc.sync.dma_start(q_raw[:], query.rearrange("(p t) q -> p t q", t=PACK))
+        nc.sync.dma_start(key_words[:].bitcast(I32), keys_words[0].rearrange("p n t -> p (n t)").bitcast(I32))
+        nc.sync.dma_start(link_lists[0][:], offs2)
+        nc.sync.dma_start(link_lists[1][:], offs3)
+        for v, vec in enumerate((sa, sb, size)):
+            nc.scalar.dma_start(rows[BLOCKS * v : BLOCKS * (v + 1), :], vec.rearrange("o (j c) -> (o j) c", c=P))
+        for j in range(E // P):
+            nc.sync.dma_start(pools[j][:], vals[j * P : (j + 1) * P, :])
+
+        ident = sbuf("ident", [P, P], F32)
+        make_identity(nc, ident[:])
+
+        warm = sbuf("warm", [P, 1], F32)
+        nc.scalar.activation(warm[:], ident[:, 0:1], ACT.Exp)
+
+        cols_ps = bank("v0", [P, P])
+        nc.tensor.transpose(cols_ps[:], rows[:], ident[:])
+        cols = sbuf("cols", [P, 3 * BLOCKS], F32)
+        nc.scalar.copy(cols[:], cols_ps[:, 0 : 3 * BLOCKS])
+        size_ps = bank("size", [P, I])
+        for j in range(BLOCKS):
+            c = 2 * BLOCKS + j
+            nc.tensor.transpose(size_ps[:, j * P : (j + 1) * P], cols[:, c : c + 1].to_broadcast([P, P]), ident[:])
+
+        ks_g = sbuf("ks_g", [P, I], U8)
+        nc.vector.tensor_copy(ks_g[:], key_scales[:].indirect(key_list[:]))
+        q_bf = sbuf("q_bf", [P, Q, PACK], BF16)
+        nc.vector.tensor_copy(q_bf[:], q_raw[:].rearrange("p t q -> p q t"))
+        q_codes = sbuf("q_codes", [P, Q], U32)
+        q_scales = sbuf("q_scales", [P, Q], U8)
+        nc.vector.quantize_mx(out=q_codes[:].bitcast(FP8X4), scales=q_scales[:], in_=q_bf[:].rearrange("p q t -> p (q t)"))
+
+        a = sbuf("a", [P, I], F32)
+        for h in range(2):
+            kw_g = sbuf(f"kw_g{h}", [P, HALF], U32)
+            nc.vector.tensor_copy(kw_g[:], key_words[:].indirect(half_list(key_list, h)))
+            a_ps = bank(f"a{h}", [P, HALF])
+            nc.tensor.matmul_mx(out=a_ps[:], lhsT=q_codes[:].bitcast(FP8X4), lhsT_scale=q_scales[:],
+                                rhs=kw_g[:].bitcast(FP8X4), rhs_scale=ks_g[:, h * HALF : (h + 1) * HALF], start=True, stop=True)
+            nc.scalar.copy(a[:, h * HALF : (h + 1) * HALF], a_ps[:])
+
+        terms = [sbuf(f"term{k}", [P, BLOCKS, Q], F32) for k in range(3)]
+        at_ps = bank("t0", [P, BLOCKS, Q])
+        for j in range(BLOCKS):
+            nc.tensor.transpose(at_ps[:, j, :], a[:, j * P : (j + 1) * P], ident[:])
+        nc.scalar.copy(terms[0][:], at_ps[:])
+        s_ps = bank("s", [P, I])
+        for j in range(BLOCKS):
+            nc.tensor.matmul(s_ps[:, j * P : (j + 1) * P], terms[0][:, j, :], ident[:], is_transpose=True, start=(j == 0), stop=False)
+        tags = ("t1", "a0", "a1", "t0")
+        for l in range(2):
+            for h in range(2):
+                looked = sbuf(f"looked{l}{h}", [P, HALF], F32)
+                nc.vector.tensor_copy(looked[:], a[:].indirect(half_list(link_lists[l], h)))
+                lt_ps = bank(tags[2 * l + h], [P, 2, Q])
+                for b in range(2):
+                    nc.tensor.transpose(lt_ps[:, b, :], looked[:, b * P : (b + 1) * P], ident[:])
+                for b in range(2):
+                    j = 2 * h + b
+                    c = BLOCKS * l + j
+                    nc.scalar.activation(terms[1 + l][:, j, :], lt_ps[:, b, :], ACT.Copy, scale=cols[:, c : c + 1])
+                for b in range(2):
+                    j = 2 * h + b
+                    nc.tensor.matmul(s_ps[:, j * P : (j + 1) * P], terms[1 + l][:, j, :], ident[:], is_transpose=True,
+                                     start=False, stop=(l == 1 and j == BLOCKS - 1))
+
+        v_codes = sbuf("v_codes", [P, E], U32)
+        v_scales = sbuf("v_scales", [P, E], U8)
+
+        def turn(src, tag, name):
+            words = src[:].bitcast(F32)
+            ps = bank(tag, [P, 2, P])
+            for u in range(2):
+                nc.tensor.transpose(ps[:, u, :], words[:, u : HALF : 2], ident[:])
+            grouped = sbuf(name, [P, P, PACK], BF16)
+            nc.scalar.copy(grouped[:].bitcast(F32), ps[:].rearrange("p u r -> p r u"))
+            return grouped
+
+        def gather_vals(j):
+            picked = sbuf(f"picked{j}", [P, I], BF16)
+            nc.vector.tensor_copy(picked[:], pools[j][:].indirect(key_list[:]))
+            return turn(picked, f"v{j % 2}", f"v_grouped{j}")
+
+        def quant_vals(j, grouped):
+            nc.vector.quantize_mx(out=v_codes[:, j * P : (j + 1) * P].bitcast(FP8X4), scales=v_scales[:, j * P : (j + 1) * P],
+                                  in_=grouped[:].rearrange("p r t -> p (r t)"))
+
+        g0 = gather_vals(0)
+        neg_max = sbuf("neg_max", [P, 1], F32)
+        nc.vector.tensor_reduce(neg_max[:], s_ps[:], AXIS.X, ALU.max, negate=True)
+        p = sbuf("p", [P, I], F32)
+        p_sum = sbuf("p_sum", [P, 1], F32)
+        nc.scalar.activation(p[:], s_ps[:], ACT.Exp, bias=neg_max[:], accum_out=p_sum[:])
+        g1 = gather_vals(1)
+        inv_sum = sbuf("inv_sum", [P, 1], F32)
+        nc.vector.reciprocal(inv_sum[:], p_sum[:])
+        w = sbuf("w", [P, I], BF16)
+        nc.vector.scalar_tensor_tensor(w[:], p[:], inv_sum[:], size_ps[:], ALU.mult, ALU.mult)
+        wg = turn(w, "t1", "w_grouped")
+        g2 = gather_vals(2)
+        quant_vals(0, g0)
+        quant_vals(1, g1)
+        w_codes = sbuf("w_codes", [P, Q], U32)
+        w_scales = sbuf("w_scales", [P, Q], U8)
+        nc.vector.quantize_mx(out=w_codes[:].bitcast(FP8X4), scales=w_scales[:], in_=wg[:].rearrange("p r t -> p (r t)"))
+        g3 = gather_vals(3)
+        quant_vals(2, g2)
+
+        def product(tag, spans):
+            lo, hi = spans[0][0], spans[-1][1]
+            o_ps = bank(tag, [P, hi - lo])
+            for c0, c1 in spans:
+                nc.tensor.matmul_mx(out=o_ps[:, c0 - lo : c1 - lo], lhsT=w_codes[:].bitcast(FP8X4), lhsT_scale=w_scales[:],
+                                    rhs=v_codes[:, c0:c1].bitcast(FP8X4), rhs_scale=v_scales[:, c0:c1], start=True, stop=True)
+            o_sb = sbuf("o_" + tag, [P, hi - lo], F32)
+            nc.scalar.copy(o_sb[:], o_ps[:])
+            nc.sync.dma_start(out[:, lo:hi], o_sb[:])
+
+        product("a0", [(0, 256), (256, 384)])
+        quant_vals(3, g3)
+        product("a1", [(384, 512)])

@@ -31,8 +31,8 @@ def tile_attend_neighbourscores_kernel(tc, query, keys_words, keys_scales, sa, s
         sb_pool = ctx.enter_context(tc.tile_pool(name="work", bufs=1))
         psum = ctx.enter_context(tc.psum_pool(name="psum", bufs=1))
 
-        def sbuf(name, shape, dtype):
-            return sb_pool.tile(shape, dtype, name=name, align_bytes=64)
+        def sbuf(name, shape, dtype, tag=None):
+            return sb_pool.tile(shape, dtype, name=name, tag=tag or name, align_bytes=64)
 
         def bank(tag, shape):
             return psum.tile(shape, F32, name=tag, tag=tag)
@@ -42,135 +42,155 @@ def tile_attend_neighbourscores_kernel(tc, query, keys_words, keys_scales, sa, s
 
         key_list = lists.tile([P, LIST_COLS], U16, name="key_list")
         link_lists = [lists.tile([P, LIST_COLS], U16, name=f"link_list{l}") for l in range(2)]
-        key_scales = sbuf("key_scales", [P, T], U8)
+        key_scales = sbuf("key_scales", [P, T], U8, tag="C")
         key_words = sbuf("key_words", [P, T], U32)
+        ident = sbuf("ident", [P, P], F32)
         q_raw = sbuf("q_raw", [P, PACK, Q], F32)
-        rows = sbuf("rows", [P, P], F32)
-        pools = [sbuf(f"val_pool{j}", [P, T], F32) for j in range(E // P)]
+        a = sbuf("a", [P, I + 32], F32)
 
         nc.vector.memset(key_scales[:].bitcast(I32), 0)
-        nc.vector.memset(rows[:], 0.0)
+        nc.vector.memset(a[:, I:], 0.0)
+        cols = [sbuf(f"cols{v}", [P, PACK], F32) for v in range(3)]
+        make_identity(nc, ident[:])
+
+        def load_cols(v, vec):
+            nc.sync.dma_start(cols[v][:], vec.rearrange("o (p j) -> (o p) j", j=PACK))
+
+        pools = {}
+
+        def load_vals(j, tag, pieces=1):
+            pools[j] = sbuf(f"val_pool{j}", [P, T], F32, tag=tag)
+            for c in range(0, T, T // pieces):
+                nc.sync.dma_start(pools[j][:, c : c + T // pieces], vals[j * P : (j + 1) * P, c : c + T // pieces])
+
         nc.sync.dma_start(key_list[:], offs)
         for g in range(4):
-            nc.sync.dma_start(key_scales[32 * g : 32 * g + 4, :].bitcast(I32), keys_scales[0, 4 * g : 4 * g + 4, :].bitcast(I32))
+            nc.scalar.dma_start(key_scales[32 * g : 32 * g + 4, :].bitcast(I32), keys_scales[0, 4 * g : 4 * g + 4, :].bitcast(I32))
+        load_cols(0, sa)
+        load_cols(1, sb)
         nc.sync.dma_start(q_raw[:], query.rearrange("(p t) q -> p t q", t=PACK))
         nc.sync.dma_start(key_words[:].bitcast(I32), keys_words[0].rearrange("p n t -> p (n t)").bitcast(I32))
         nc.sync.dma_start(link_lists[0][:], offs2)
+        load_vals(0, None, 2)
         nc.sync.dma_start(link_lists[1][:], offs3)
-        for v, vec in enumerate((sa, sb, size)):
-            nc.scalar.dma_start(rows[BLOCKS * v : BLOCKS * (v + 1), :], vec.rearrange("o (j c) -> (o j) c", c=P))
-        for j in range(E // P):
-            nc.sync.dma_start(pools[j][:], vals[j * P : (j + 1) * P, :])
+        load_cols(2, size)
+        load_vals(2, "B", 2)
+        load_vals(1, "F")
+        load_vals(3, "E")
 
-        ident = sbuf("ident", [P, P], F32)
-        make_identity(nc, ident[:])
-
-        warm = sbuf("warm", [P, 1], F32)
-        nc.scalar.activation(warm[:], ident[:, 0:1], ACT.Exp)
-
-        cols_ps = bank("v0", [P, P])
-        nc.tensor.transpose(cols_ps[:], rows[:], ident[:])
-        cols = sbuf("cols", [P, 3 * BLOCKS], F32)
-        nc.scalar.copy(cols[:], cols_ps[:, 0 : 3 * BLOCKS])
-        size_ps = bank("size", [P, I])
-        for j in range(BLOCKS):
-            c = 2 * BLOCKS + j
-            nc.tensor.transpose(size_ps[:, j * P : (j + 1) * P], cols[:, c : c + 1].to_broadcast([P, P]), ident[:])
-
-        ks_g = sbuf("ks_g", [P, I], U8)
-        nc.vector.tensor_copy(ks_g[:], key_scales[:].indirect(key_list[:]))
         q_bf = sbuf("q_bf", [P, Q, PACK], BF16)
         nc.vector.tensor_copy(q_bf[:], q_raw[:].rearrange("p t q -> p q t"))
+        warm = sbuf("warm", [P, 1], F32)
+        nc.scalar.activation(warm[:], q_bf[:, 0, 0:1], ACT.Exp, scale=0.0)
         q_codes = sbuf("q_codes", [P, Q], U32)
         q_scales = sbuf("q_scales", [P, Q], U8)
         nc.vector.quantize_mx(out=q_codes[:].bitcast(FP8X4), scales=q_scales[:], in_=q_bf[:].rearrange("p q t -> p (q t)"))
 
-        a = sbuf("a", [P, I], F32)
+        def spread_cols(v):
+            ps = bank(f"bc{v}", [P, PACK, P])
+            for j in range(PACK):
+                nc.tensor.transpose(ps[:, j, :], cols[v][:, j : j + 1].to_broadcast([P, P]), ident[:])
+            return ps
+
+        spread = []
+        for v in range(2):
+            ps = spread_cols(v)
+            row = sbuf(f"spread{v}", [P, P, PACK], F32)
+            nc.scalar.copy(row[:], ps[:].rearrange("p j c -> p c j"))
+            spread.append(row[:].rearrange("p c j -> p (c j)"))
+
+        ks_g = sbuf("ks_g", [P, I], U8)
+        nc.vector.tensor_copy(ks_g[:], key_scales[:].indirect(key_list[:]))
+        kw_g = [sbuf("kw_g0", [P, HALF], U32, tag="C"), sbuf("kw_g1", [P, HALF], U32)]
         for h in range(2):
-            kw_g = sbuf(f"kw_g{h}", [P, HALF], U32)
-            nc.vector.tensor_copy(kw_g[:], key_words[:].indirect(half_list(key_list, h)))
-            a_ps = bank(f"a{h}", [P, HALF])
+            nc.vector.tensor_copy(kw_g[h][:], key_words[:].indirect(half_list(key_list, h)))
+
+        for h in range(2):
+            a_ps = bank(f"bc{h}", [P, HALF])
             nc.tensor.matmul_mx(out=a_ps[:], lhsT=q_codes[:].bitcast(FP8X4), lhsT_scale=q_scales[:],
-                                rhs=kw_g[:].bitcast(FP8X4), rhs_scale=ks_g[:, h * HALF : (h + 1) * HALF], start=True, stop=True)
-            nc.scalar.copy(a[:, h * HALF : (h + 1) * HALF], a_ps[:])
+                                rhs=kw_g[h][:].bitcast(FP8X4), rhs_scale=ks_g[:, h * HALF : (h + 1) * HALF], start=True, stop=True)
+            nc.vector.tensor_copy(a[:, h * HALF : (h + 1) * HALF], a_ps[:])
 
-        terms = [sbuf(f"term{k}", [P, BLOCKS, Q], F32) for k in range(3)]
-        at_ps = bank("t0", [P, BLOCKS, Q])
-        for j in range(BLOCKS):
-            nc.tensor.transpose(at_ps[:, j, :], a[:, j * P : (j + 1) * P], ident[:])
-        nc.scalar.copy(terms[0][:], at_ps[:])
-        s_ps = bank("s", [P, I])
-        for j in range(BLOCKS):
-            nc.tensor.matmul(s_ps[:, j * P : (j + 1) * P], terms[0][:, j, :], ident[:], is_transpose=True, start=(j == 0), stop=False)
-        tags = ("t1", "a0", "a1", "t0")
-        for l in range(2):
-            for h in range(2):
-                looked = sbuf(f"looked{l}{h}", [P, HALF], F32)
-                nc.vector.tensor_copy(looked[:], a[:].indirect(half_list(link_lists[l], h)))
-                lt_ps = bank(tags[2 * l + h], [P, 2, Q])
-                for b in range(2):
-                    nc.tensor.transpose(lt_ps[:, b, :], looked[:, b * P : (b + 1) * P], ident[:])
-                for b in range(2):
-                    j = 2 * h + b
-                    c = BLOCKS * l + j
-                    nc.scalar.activation(terms[1 + l][:, j, :], lt_ps[:, b, :], ACT.Copy, scale=cols[:, c : c + 1])
-                for b in range(2):
-                    j = 2 * h + b
-                    nc.tensor.matmul(s_ps[:, j * P : (j + 1) * P], terms[1 + l][:, j, :], ident[:], is_transpose=True,
-                                     start=False, stop=(l == 1 and j == BLOCKS - 1))
+        size_ps = spread_cols(2)
 
-        v_codes = sbuf("v_codes", [P, E], U32)
-        v_scales = sbuf("v_scales", [P, E], U8)
-
-        def turn(src, tag, name):
+        def turn(src, tag, name, sb_tag=None):
             words = src[:].bitcast(F32)
             ps = bank(tag, [P, 2, P])
             for u in range(2):
                 nc.tensor.transpose(ps[:, u, :], words[:, u : HALF : 2], ident[:])
-            grouped = sbuf(name, [P, P, PACK], BF16)
+            grouped = sbuf(name, [P, P, PACK], BF16, tag=sb_tag)
             nc.scalar.copy(grouped[:].bitcast(F32), ps[:].rearrange("p u r -> p r u"))
             return grouped
 
-        def gather_vals(j):
-            picked = sbuf(f"picked{j}", [P, I], BF16)
+        def cast_vals(j, tag):
+            pool_bf = sbuf(f"val_bf{j}", [P, T], BF16, tag=tag)
+            for c in range(0, T, T // 2):
+                nc.scalar.activation(pool_bf[:, c : c + T // 2], pools[j][:, c : c + T // 2], ACT.Copy)
+            return pool_bf
+
+        def gather_scalar(j, pool_bf, tag):
+            picked = sbuf(f"picked{j}", [P, I], BF16, tag=tag)
+            nc.scalar.activation(picked[:], pool_bf[:].indirect(key_list[:]), ACT.Copy)
+            return picked
+
+        def gather_vector(j, tag):
+            picked = sbuf(f"picked{j}", [P, I], BF16, tag=tag)
             nc.vector.tensor_copy(picked[:], pools[j][:].indirect(key_list[:]))
-            return turn(picked, f"v{j % 2}", f"v_grouped{j}")
+            return picked
+
+        g0 = turn(gather_scalar(0, cast_vals(0, "cols1"), None), "v0", "v_grouped0")
+        bf2 = cast_vals(2, None)
+
+        linked = []
+        for l in range(2):
+            g = sbuf(f"linked{l}", [P, I], F32)
+            nc.vector.tensor_tensor(g[:], a[:].indirect(link_lists[l][:]), spread[l], ALU.mult)
+            linked.append(g)
+        part = sbuf("part", [P, I], F32)
+        nc.vector.tensor_tensor(part[:], linked[0][:], a[:, 0:I], ALU.add)
+        s = sbuf("s", [P, I], F32)
+        nc.vector.tensor_tensor(s[:], part[:], linked[1][:], ALU.add)
+        neg_max = sbuf("neg_max", [P, 1], F32)
+        nc.vector.tensor_reduce(neg_max[:], s[:], AXIS.X, ALU.max, negate=True)
+        p = sbuf("p", [P, I], F32, tag="B")
+        p_sum = sbuf("p_sum", [P, 1], F32)
+        nc.scalar.activation(p[:], s[:], ACT.Exp, bias=neg_max[:], accum_out=p_sum[:])
+        picked1 = gather_vector(1, "part")
+        picked2 = gather_scalar(2, bf2, "s")
+        g1 = turn(picked1, "v1", "v_grouped1", "val_bf2")
+        inv_sum = sbuf("inv_sum", [P, 1], F32, tag="F")
+        nc.vector.reciprocal(inv_sum[:], p_sum[:])
+        w = sbuf("w", [P, I], BF16)
+        nc.vector.scalar_tensor_tensor(w[:].rearrange("p (c j) -> p c j", j=PACK), p[:].rearrange("p (c j) -> p c j", j=PACK),
+                                       inv_sum[:], size_ps[:].rearrange("p j c -> p c j"), ALU.mult, ALU.mult)
+        wg = turn(w, "a1", "w_grouped")
+        g2 = turn(picked2, "a0", "v_grouped2")
+        picked3 = gather_vector(3, "B")
+        g3 = turn(picked3, "x", "v_grouped3")
+
+        v_codes = sbuf("v_codes", [P, E], U32)
+        v_scales = sbuf("v_scales", [P, E], U8, tag="E")
 
         def quant_vals(j, grouped):
             nc.vector.quantize_mx(out=v_codes[:, j * P : (j + 1) * P].bitcast(FP8X4), scales=v_scales[:, j * P : (j + 1) * P],
                                   in_=grouped[:].rearrange("p r t -> p (r t)"))
 
-        g0 = gather_vals(0)
-        neg_max = sbuf("neg_max", [P, 1], F32)
-        nc.vector.tensor_reduce(neg_max[:], s_ps[:], AXIS.X, ALU.max, negate=True)
-        p = sbuf("p", [P, I], F32)
-        p_sum = sbuf("p_sum", [P, 1], F32)
-        nc.scalar.activation(p[:], s_ps[:], ACT.Exp, bias=neg_max[:], accum_out=p_sum[:])
-        g1 = gather_vals(1)
-        inv_sum = sbuf("inv_sum", [P, 1], F32)
-        nc.vector.reciprocal(inv_sum[:], p_sum[:])
-        w = sbuf("w", [P, I], BF16)
-        nc.vector.scalar_tensor_tensor(w[:], p[:], inv_sum[:], size_ps[:], ALU.mult, ALU.mult)
-        wg = turn(w, "t1", "w_grouped")
-        g2 = gather_vals(2)
-        quant_vals(0, g0)
-        quant_vals(1, g1)
-        w_codes = sbuf("w_codes", [P, Q], U32)
-        w_scales = sbuf("w_scales", [P, Q], U8)
-        nc.vector.quantize_mx(out=w_codes[:].bitcast(FP8X4), scales=w_scales[:], in_=wg[:].rearrange("p r t -> p (r t)"))
-        g3 = gather_vals(3)
-        quant_vals(2, g2)
-
-        def product(tag, spans):
+        def product(tag, spans, copy):
             lo, hi = spans[0][0], spans[-1][1]
             o_ps = bank(tag, [P, hi - lo])
             for c0, c1 in spans:
                 nc.tensor.matmul_mx(out=o_ps[:, c0 - lo : c1 - lo], lhsT=w_codes[:].bitcast(FP8X4), lhsT_scale=w_scales[:],
                                     rhs=v_codes[:, c0:c1].bitcast(FP8X4), rhs_scale=v_scales[:, c0:c1], start=True, stop=True)
             o_sb = sbuf("o_" + tag, [P, hi - lo], F32)
-            nc.scalar.copy(o_sb[:], o_ps[:])
+            copy(o_sb[:], o_ps[:])
             nc.sync.dma_start(out[:, lo:hi], o_sb[:])
 
-        product("a0", [(0, 256), (256, 384)])
+        quant_vals(0, g0)
+        quant_vals(1, g1)
+        w_codes = sbuf("w_codes", [P, Q], U32)
+        w_scales = sbuf("w_scales", [P, Q], U8)
+        nc.vector.quantize_mx(out=w_codes[:].bitcast(FP8X4), scales=w_scales[:], in_=wg[:].rearrange("p r t -> p (r t)"))
+        quant_vals(2, g2)
+        product("bc0", [(0, 256), (256, 384)], nc.scalar.copy)
         quant_vals(3, g3)
-        product("a1", [(384, 512)])
+        product("bc1", [(384, 512)], nc.vector.tensor_copy)

@@ -48,7 +48,8 @@ def tile_attend_neighbourscores_kernel(tc, query, keys_words, keys_scales, sa, s
         q_raw = sbuf("q_raw", [P, PACK, Q], F32)
         a = sbuf("a", [P, I + 32], F32)
 
-        nc.vector.memset(key_scales[:].bitcast(I32), 0)
+        nc.vector.memset(key_scales[:, 0 : T // 2].bitcast(I32), 0)
+        nc.gpsimd.memset(key_scales[:, T // 2 : T].bitcast(I32), 0)
         nc.vector.memset(a[:, I:], 0.0)
         cols = [sbuf(f"cols{v}", [P, PACK], F32) for v in range(3)]
         make_identity(nc, ident[:])
@@ -63,15 +64,18 @@ def tile_attend_neighbourscores_kernel(tc, query, keys_words, keys_scales, sa, s
             for c in range(0, T, T // pieces):
                 nc.sync.dma_start(pools[j][:, c : c + T // pieces], vals[j * P : (j + 1) * P, c : c + T // pieces])
 
+        def load_scales(g, queue):
+            queue.dma_start(key_scales[32 * g : 32 * g + 4, :].bitcast(I32), keys_scales[0, 4 * g : 4 * g + 4, :].bitcast(I32))
+
         nc.sync.dma_start(key_list[:], offs)
-        for g in range(4):
-            nc.scalar.dma_start(key_scales[32 * g : 32 * g + 4, :].bitcast(I32), keys_scales[0, 4 * g : 4 * g + 4, :].bitcast(I32))
-        load_cols(0, sa)
-        load_cols(1, sb)
         nc.sync.dma_start(q_raw[:], query.rearrange("(p t) q -> p t q", t=PACK))
+        load_cols(0, sa)
+        for g in range(4):
+            load_scales(g, nc.sync if g < 2 else nc.scalar)
         nc.sync.dma_start(key_words[:].bitcast(I32), keys_words[0].rearrange("p n t -> p (n t)").bitcast(I32))
+        load_cols(1, sb)
         nc.sync.dma_start(link_lists[0][:], offs2)
-        load_vals(0, None, 2)
+        load_vals(0, "A", 2)
         nc.sync.dma_start(link_lists[1][:], offs3)
         load_cols(2, size)
         load_vals(2, "B", 2)
@@ -86,18 +90,16 @@ def tile_attend_neighbourscores_kernel(tc, query, keys_words, keys_scales, sa, s
         q_scales = sbuf("q_scales", [P, Q], U8)
         nc.vector.quantize_mx(out=q_codes[:].bitcast(FP8X4), scales=q_scales[:], in_=q_bf[:].rearrange("p q t -> p (q t)"))
 
-        def spread_cols(v):
-            ps = bank(f"bc{v}", [P, PACK, P])
-            for j in range(PACK):
-                nc.tensor.transpose(ps[:, j, :], cols[v][:, j : j + 1].to_broadcast([P, P]), ident[:])
+        def spread_cols(v, tag, js):
+            ps = bank(tag, [P, len(js), P])
+            for n, j in enumerate(js):
+                nc.tensor.transpose(ps[:, n, :], cols[v][:, j : j + 1].to_broadcast([P, P]), ident[:])
             return ps
 
-        spread = []
-        for v in range(2):
-            ps = spread_cols(v)
-            row = sbuf(f"spread{v}", [P, P, PACK], F32)
-            nc.scalar.copy(row[:], ps[:].rearrange("p j c -> p c j"))
-            spread.append(row[:].rearrange("p c j -> p (c j)"))
+        sa_row = sbuf("sa_row", [P, P, PACK], F32)
+        for h in range(2):
+            ps = spread_cols(0, f"bc{h}", (2 * h, 2 * h + 1))
+            nc.scalar.copy(sa_row[:, :, 2 * h : 2 * h + 2], ps[:].rearrange("p j c -> p c j"))
 
         ks_g = sbuf("ks_g", [P, I], U8)
         nc.vector.tensor_copy(ks_g[:], key_scales[:].indirect(key_list[:]))
@@ -111,7 +113,8 @@ def tile_attend_neighbourscores_kernel(tc, query, keys_words, keys_scales, sa, s
                                 rhs=kw_g[h][:].bitcast(FP8X4), rhs_scale=ks_g[:, h * HALF : (h + 1) * HALF], start=True, stop=True)
             nc.vector.tensor_copy(a[:, h * HALF : (h + 1) * HALF], a_ps[:])
 
-        size_ps = spread_cols(2)
+        sb_ps = spread_cols(1, "bc1", range(PACK))
+        size_ps = spread_cols(2, "bc2", range(PACK))
 
         def turn(src, tag, name, sb_tag=None):
             words = src[:].bitcast(F32)
@@ -138,18 +141,21 @@ def tile_attend_neighbourscores_kernel(tc, query, keys_words, keys_scales, sa, s
             nc.vector.tensor_copy(picked[:], pools[j][:].indirect(key_list[:]))
             return picked
 
-        g0 = turn(gather_scalar(0, cast_vals(0, "cols1"), None), "v0", "v_grouped0")
-        bf2 = cast_vals(2, None)
+        bf0 = cast_vals(0, None)
+        sb_row = sbuf("sb_row", [P, P, PACK], F32, tag="A")
+        nc.scalar.copy(sb_row[:], sb_ps[:].rearrange("p j c -> p c j"))
+        picked0 = gather_scalar(0, bf0, "cols1")
+        bf2 = cast_vals(2, "cols2")
 
-        linked = []
-        for l in range(2):
+        def linked(l, strength):
             g = sbuf(f"linked{l}", [P, I], F32)
-            nc.vector.tensor_tensor(g[:], a[:].indirect(link_lists[l][:]), spread[l], ALU.mult)
-            linked.append(g)
+            nc.vector.tensor_tensor(g[:], a[:].indirect(link_lists[l][:]), strength[:].rearrange("p c j -> p (c j)"), ALU.mult)
+            return g
+
         part = sbuf("part", [P, I], F32)
-        nc.vector.tensor_tensor(part[:], linked[0][:], a[:, 0:I], ALU.add)
+        nc.vector.tensor_tensor(part[:], linked(0, sa_row)[:], a[:, 0:I], ALU.add)
         s = sbuf("s", [P, I], F32)
-        nc.vector.tensor_tensor(s[:], part[:], linked[1][:], ALU.add)
+        nc.vector.tensor_tensor(s[:], part[:], linked(1, sb_row)[:], ALU.add)
         neg_max = sbuf("neg_max", [P, 1], F32)
         nc.vector.tensor_reduce(neg_max[:], s[:], AXIS.X, ALU.max, negate=True)
         p = sbuf("p", [P, I], F32, tag="B")
@@ -157,7 +163,8 @@ def tile_attend_neighbourscores_kernel(tc, query, keys_words, keys_scales, sa, s
         nc.scalar.activation(p[:], s[:], ACT.Exp, bias=neg_max[:], accum_out=p_sum[:])
         picked1 = gather_vector(1, "part")
         picked2 = gather_scalar(2, bf2, "s")
-        g1 = turn(picked1, "v1", "v_grouped1", "val_bf2")
+        g0 = turn(picked0, "v0", "v_grouped0", "neg_max")
+        g1 = turn(picked1, "v1", "v_grouped1", "cols2")
         inv_sum = sbuf("inv_sum", [P, 1], F32, tag="F")
         nc.vector.reciprocal(inv_sum[:], p_sum[:])
         w = sbuf("w", [P, I], BF16)

@@ -52,11 +52,12 @@ def tile_attend_neighbourscores_kernel(tc, query, keys_words, keys_scales, sa, s
         nc.gpsimd.memset(key_scales[:, T // 2 : T].bitcast(I32), 0)
         nc.vector.memset(a[:, I:], 0.0)
         cols = [sbuf(f"cols{v}", [P, PACK], F32) for v in range(3)]
+
+        def load_cols(v, vec, queue):
+            queue.dma_start(cols[v][:], vec.rearrange("o (p j) -> (o p) j", j=PACK))
+
+        load_cols(1, sb, nc.gpsimd)
         make_identity(nc, ident[:])
-
-        def load_cols(v, vec):
-            nc.sync.dma_start(cols[v][:], vec.rearrange("o (p j) -> (o p) j", j=PACK))
-
         pools = {}
 
         def load_vals(j, tag, pieces=1):
@@ -69,37 +70,36 @@ def tile_attend_neighbourscores_kernel(tc, query, keys_words, keys_scales, sa, s
 
         nc.sync.dma_start(key_list[:], offs)
         nc.sync.dma_start(q_raw[:], query.rearrange("(p t) q -> p t q", t=PACK))
-        load_cols(0, sa)
+        load_cols(0, sa, nc.sync)
         for g in range(4):
             load_scales(g, nc.sync if g < 2 else nc.scalar)
         nc.sync.dma_start(key_words[:].bitcast(I32), keys_words[0].rearrange("p n t -> p (n t)").bitcast(I32))
-        load_cols(1, sb)
         nc.sync.dma_start(link_lists[0][:], offs2)
-        load_vals(0, "A", 2)
+        load_vals(0, None, 2)
         nc.sync.dma_start(link_lists[1][:], offs3)
-        load_cols(2, size)
+        load_cols(2, size, nc.sync)
         load_vals(2, "B", 2)
         load_vals(1, "F")
         load_vals(3, "E")
 
         q_bf = sbuf("q_bf", [P, Q, PACK], BF16)
         nc.vector.tensor_copy(q_bf[:], q_raw[:].rearrange("p t q -> p q t"))
-        warm = sbuf("warm", [P, 1], F32)
-        nc.scalar.activation(warm[:], q_bf[:, 0, 0:1], ACT.Exp, scale=0.0)
         q_codes = sbuf("q_codes", [P, Q], U32)
         q_scales = sbuf("q_scales", [P, Q], U8)
         nc.vector.quantize_mx(out=q_codes[:].bitcast(FP8X4), scales=q_scales[:], in_=q_bf[:].rearrange("p q t -> p (q t)"))
 
-        def spread_cols(v, tag, js):
-            ps = bank(tag, [P, len(js), P])
-            for n, j in enumerate(js):
+        def spread_cols(v, tag, places):
+            ps = bank(tag, [P, len(places), P])
+            for n, j in enumerate(places):
                 nc.tensor.transpose(ps[:, n, :], cols[v][:, j : j + 1].to_broadcast([P, P]), ident[:])
             return ps
 
-        sa_row = sbuf("sa_row", [P, P, PACK], F32)
+        strengths = [sbuf(f"strength{v}", [P, P, PACK], F32) for v in range(2)]
         for h in range(2):
             ps = spread_cols(0, f"bc{h}", (2 * h, 2 * h + 1))
-            nc.scalar.copy(sa_row[:, :, 2 * h : 2 * h + 2], ps[:].rearrange("p j c -> p c j"))
+            nc.scalar.activation(strengths[0][:, :, 2 * h : 2 * h + 2], ps[:].rearrange("p j c -> p c j"), ACT.Copy)
+        ps = spread_cols(1, "bc2", range(PACK))
+        nc.scalar.copy(strengths[1][:], ps[:].rearrange("p j c -> p c j"))
 
         ks_g = sbuf("ks_g", [P, I], U8)
         nc.vector.tensor_copy(ks_g[:], key_scales[:].indirect(key_list[:]))
@@ -113,8 +113,7 @@ def tile_attend_neighbourscores_kernel(tc, query, keys_words, keys_scales, sa, s
                                 rhs=kw_g[h][:].bitcast(FP8X4), rhs_scale=ks_g[:, h * HALF : (h + 1) * HALF], start=True, stop=True)
             nc.vector.tensor_copy(a[:, h * HALF : (h + 1) * HALF], a_ps[:])
 
-        sb_ps = spread_cols(1, "bc1", range(PACK))
-        size_ps = spread_cols(2, "bc2", range(PACK))
+        size_ps = spread_cols(2, "bc0", range(PACK))
 
         def turn(src, tag, name, sb_tag=None):
             words = src[:].bitcast(F32)
@@ -141,21 +140,21 @@ def tile_attend_neighbourscores_kernel(tc, query, keys_words, keys_scales, sa, s
             nc.vector.tensor_copy(picked[:], pools[j][:].indirect(key_list[:]))
             return picked
 
-        bf0 = cast_vals(0, None)
-        sb_row = sbuf("sb_row", [P, P, PACK], F32, tag="A")
-        nc.scalar.copy(sb_row[:], sb_ps[:].rearrange("p j c -> p c j"))
-        picked0 = gather_scalar(0, bf0, "cols1")
+        picked0 = gather_scalar(0, cast_vals(0, "cols1"), None)
         bf2 = cast_vals(2, "cols2")
 
-        def linked(l, strength):
-            g = sbuf(f"linked{l}", [P, I], F32)
-            nc.vector.tensor_tensor(g[:], a[:].indirect(link_lists[l][:]), strength[:].rearrange("p c j -> p (c j)"), ALU.mult)
-            return g
-
+        flat = [row[:].rearrange("p c j -> p (c j)") for row in strengths]
+        link0 = sbuf("link0", [P, I], F32)
+        link1 = sbuf("link1", [P, I], F32)
         part = sbuf("part", [P, I], F32)
-        nc.vector.tensor_tensor(part[:], linked(0, sa_row)[:], a[:, 0:I], ALU.add)
         s = sbuf("s", [P, I], F32)
-        nc.vector.tensor_tensor(s[:], part[:], linked(1, sb_row)[:], ALU.add)
+        halves = [slice(h * HALF, (h + 1) * HALF) for h in range(2)]
+        nc.vector.tensor_tensor(link0[:], a[:].indirect(link_lists[0][:]), flat[0], ALU.mult)
+        nc.vector.tensor_tensor(link1[:, halves[0]], a[:].indirect(half_list(link_lists[1], 0)), flat[1][:, halves[0]], ALU.mult)
+        nc.vector.tensor_tensor(part[:], link0[:], a[:, 0:I], ALU.add)
+        nc.vector.tensor_tensor(link1[:, halves[1]], a[:].indirect(half_list(link_lists[1], 1)), flat[1][:, halves[1]], ALU.mult)
+        for cs in halves:
+            nc.vector.tensor_tensor(s[:, cs], part[:, cs], link1[:, cs], ALU.add)
         neg_max = sbuf("neg_max", [P, 1], F32)
         nc.vector.tensor_reduce(neg_max[:], s[:], AXIS.X, ALU.max, negate=True)
         p = sbuf("p", [P, I], F32, tag="B")
@@ -172,7 +171,7 @@ def tile_attend_neighbourscores_kernel(tc, query, keys_words, keys_scales, sa, s
                                        inv_sum[:], size_ps[:].rearrange("p j c -> p c j"), ALU.mult, ALU.mult)
         wg = turn(w, "a1", "w_grouped")
         g2 = turn(picked2, "a0", "v_grouped2")
-        picked3 = gather_vector(3, "B")
+        picked3 = gather_vector(3, "p_sum")
         g3 = turn(picked3, "x", "v_grouped3")
 
         v_codes = sbuf("v_codes", [P, E], U32)
@@ -198,6 +197,6 @@ def tile_attend_neighbourscores_kernel(tc, query, keys_words, keys_scales, sa, s
         w_scales = sbuf("w_scales", [P, Q], U8)
         nc.vector.quantize_mx(out=w_codes[:].bitcast(FP8X4), scales=w_scales[:], in_=wg[:].rearrange("p r t -> p (r t)"))
         quant_vals(2, g2)
-        product("bc0", [(0, 256), (256, 384)], nc.scalar.copy)
+        product("bc2", [(0, 256), (256, 384)], nc.scalar.copy)
         quant_vals(3, g3)
         product("bc1", [(384, 512)], nc.vector.tensor_copy)

from contextlib import ExitStack

import concourse.mybir as mybir
from concourse.masks import make_identity

D, T, I, Q, E = 512, 2048, 512, 128, 512
FLOPS = 2 * D * Q * I + 2 * I * Q * E

F32 = mybir.dt.float32
BF16 = mybir.dt.bfloat16
I32 = mybir.dt.int32
U32 = mybir.dt.uint32
U16 = mybir.dt.uint16
U8 = mybir.dt.uint8
FP8X4 = mybir.dt.float8_e4m3fn_x4
ALU = mybir.AluOpType
ACT = mybir.ActivationFunctionType
AXIS = mybir.AxisListType

P = 128
PACK = 4
BLOCKS = I // P
HALF = I // 2
LIST_COLS = I // 16


def tile_attend_neighbourscores_kernel(tc, query, keys_words, keys_scales, sa, sb, size, vals, offs, offs2, offs3, out):
    nc = tc.nc
    with ExitStack() as ctx:
        lists = ctx.enter_context(tc.tile_pool(name="lists", bufs=1))
        sb_pool = ctx.enter_context(tc.tile_pool(name="work", bufs=1))
        psum = ctx.enter_context(tc.psum_pool(name="psum", bufs=1))

        def sbuf(name, shape, dtype, tag=None):
            return sb_pool.tile(shape, dtype, name=name, tag=tag or name, align_bytes=64)

        def bank(tag, shape):
            return psum.tile(shape, F32, name=tag, tag=tag)

        def half_list(tile, h):
            return tile[:, h * LIST_COLS // 2 : (h + 1) * LIST_COLS // 2]

        key_list = lists.tile([P, LIST_COLS], U16, name="key_list")
        link_lists = [lists.tile([P, LIST_COLS], U16, name=f"link_list{l}") for l in range(2)]
        key_scales = sbuf("key_scales", [P, T], U8, tag="C")
        key_words = sbuf("key_words", [P, T], U32)
        ident = sbuf("ident", [P, P], F32)
        q_raw = sbuf("q_raw", [P, PACK, Q], F32)
        a = sbuf("a", [P, I + 32], F32)

        nc.vector.memset(key_scales[:, 0 : T // 2].bitcast(I32), 0)
        nc.gpsimd.memset(key_scales[:, T // 2 : T].bitcast(I32), 0)
        nc.vector.memset(a[:, I:], 0.0)
        cols = [sbuf(f"cols{v}", [P, PACK], F32) for v in range(3)]

        def load_cols(v, vec, queue):
            queue.dma_start(cols[v][:], vec.rearrange("o (p j) -> (o p) j", j=PACK))

        load_cols(1, sb, nc.gpsimd)
        make_identity(nc, ident[:])
        pools = {}

        def load_vals(j, tag, pieces=1):
            pools[j] = sbuf(f"val_pool{j}", [P, T], F32, tag=tag)
            for c in range(0, T, T // pieces):
                nc.sync.dma_start(pools[j][:, c : c + T // pieces], vals[j * P : (j + 1) * P, c : c + T // pieces])

        def load_scales(g, queue):
            queue.dma_start(key_scales[32 * g : 32 * g + 4, :].bitcast(I32), keys_scales[0, 4 * g : 4 * g + 4, :].bitcast(I32))

        nc.sync.dma_start(key_list[:], offs)
        nc.sync.dma_start(q_raw[:], query.rearrange("(p t) q -> p t q", t=PACK))
        load_cols(0, sa, nc.sync)
        for g in range(4):
            load_scales(g, nc.sync if g < 2 else nc.scalar)
        nc.sync.dma_start(key_words[:].bitcast(I32), keys_words[0].rearrange("p n t -> p (n t)").bitcast(I32))
        nc.sync.dma_start(link_lists[0][:], offs2)
        load_vals(0, None, 2)
        nc.sync.dma_start(link_lists[1][:], offs3)
        load_cols(2, size, nc.sync)
        load_vals(2, "B", 2)
        load_vals(1, "F")
        load_vals(3, "E")

        q_bf = sbuf("q_bf", [P, Q, PACK], BF16)
        nc.vector.tensor_copy(q_bf[:], q_raw[:].rearrange("p t q -> p q t"))
        q_codes = sbuf("q_codes", [P, Q], U32)
        q_scales = sbuf("q_scales", [P, Q], U8)
        nc.vector.quantize_mx(out=q_codes[:].bitcast(FP8X4), scales=q_scales[:], in_=q_bf[:].rearrange("p q t -> p (q t)"))

        def spread_cols(v, tag, places):
            ps = bank(tag, [P, len(places), P])
            for n, j in enumerate(places):
                nc.tensor.transpose(ps[:, n, :], cols[v][:, j : j + 1].to_broadcast([P, P]), ident[:])
            return ps

        strengths = [sbuf(f"strength{v}", [P, P, PACK], F32) for v in range(2)]
        for h in range(2):
            ps = spread_cols(0, f"bc{h}", (2 * h, 2 * h + 1))
            nc.scalar.activation(strengths[0][:, :, 2 * h : 2 * h + 2], ps[:].rearrange("p j c -> p c j"), ACT.Copy)
        ps = spread_cols(1, "bc2", range(PACK))
        nc.scalar.copy(strengths[1][:], ps[:].rearrange("p j c -> p c j"))

        ks_g = sbuf("ks_g", [P, I], U8)
        nc.vector.tensor_copy(ks_g[:], key_scales[:].indirect(key_list[:]))
        kw_g = [sbuf("kw_g0", [P, HALF], U32, tag="C"), sbuf("kw_g1", [P, HALF], U32)]
        for h in range(2):
            nc.vector.tensor_copy(kw_g[h][:], key_words[:].indirect(half_list(key_list, h)))

        for h in range(2):
            a_ps = bank(f"bc{h}", [P, HALF])
            nc.tensor.matmul_mx(out=a_ps[:], lhsT=q_codes[:].bitcast(FP8X4), lhsT_scale=q_scales[:],
                                rhs=kw_g[h][:].bitcast(FP8X4), rhs_scale=ks_g[:, h * HALF : (h + 1) * HALF], start=True, stop=True)
            nc.vector.tensor_copy(a[:, h * HALF : (h + 1) * HALF], a_ps[:])

        size_ps = spread_cols(2, "bc0", range(PACK))

        def turn(src, tag, name, sb_tag=None):
            words = src[:].bitcast(F32)
            ps = bank(tag, [P, 2, P])
            for u in range(2):
                nc.tensor.transpose(ps[:, u, :], words[:, u : HALF : 2], ident[:])
            grouped = sbuf(name, [P, P, PACK], BF16, tag=sb_tag)
            nc.scalar.copy(grouped[:].bitcast(F32), ps[:].rearrange("p u r -> p r u"))
            return grouped

        def cast_vals(j, tag):
            pool_bf = sbuf(f"val_bf{j}", [P, T], BF16, tag=tag)
            for c in range(0, T, T // 2):
                nc.scalar.activation(pool_bf[:, c : c + T // 2], pools[j][:, c : c + T // 2], ACT.Copy)
            return pool_bf

        def gather_scalar(j, pool_bf, tag):
            picked = sbuf(f"picked{j}", [P, I], BF16, tag=tag)
            nc.scalar.activation(picked[:], pool_bf[:].indirect(key_list[:]), ACT.Copy)
            return picked

        def gather_vector(j, tag):
            picked = sbuf(f"picked{j}", [P, I], BF16, tag=tag)
            nc.vector.tensor_copy(picked[:], pools[j][:].indirect(key_list[:]))
            return picked

        picked0 = gather_scalar(0, cast_vals(0, "cols1"), None)
        bf2 = cast_vals(2, "cols2")

        flat = [row[:].rearrange("p c j -> p (c j)") for row in strengths]
        link0 = sbuf("link0", [P, I], F32)
        link1 = sbuf("link1", [P, I], F32)
        part = sbuf("part", [P, I], F32)
        s = sbuf("s", [P, I], F32)
        halves = [slice(h * HALF, (h + 1) * HALF) for h in range(2)]
        nc.vector.tensor_tensor(link0[:], a[:].indirect(link_lists[0][:]), flat[0], ALU.mult)
        nc.vector.tensor_tensor(link1[:, halves[0]], a[:].indirect(half_list(link_lists[1], 0)), flat[1][:, halves[0]], ALU.mult)
        nc.vector.tensor_tensor(part[:], link0[:], a[:, 0:I], ALU.add)
        nc.vector.tensor_tensor(link1[:, halves[1]], a[:].indirect(half_list(link_lists[1], 1)), flat[1][:, halves[1]], ALU.mult)
        for cs in halves:
            nc.vector.tensor_tensor(s[:, cs], part[:, cs], link1[:, cs], ALU.add)
        neg_max = sbuf("neg_max", [P, 1], F32)
        nc.vector.tensor_reduce(neg_max[:], s[:], AXIS.X, ALU.max, negate=True)
        p = sbuf("p", [P, I], F32, tag="B")
        p_sum = sbuf("p_sum", [P, 1], F32)
        nc.scalar.activation(p[:], s[:], ACT.Exp, bias=neg_max[:], accum_out=p_sum[:])
        picked1 = gather_vector(1, "part")
        picked2 = gather_scalar(2, bf2, "s")
        g0 = turn(picked0, "v0", "v_grouped0", "neg_max")
        g1 = turn(picked1, "v1", "v_grouped1", "cols2")
        inv_sum = sbuf("inv_sum", [P, 1], F32, tag="F")
        nc.vector.reciprocal(inv_sum[:], p_sum[:])
        w = sbuf("w", [P, I], BF16)
        nc.vector.scalar_tensor_tensor(w[:].rearrange("p (c j) -> p c j", j=PACK), p[:].rearrange("p (c j) -> p c j", j=PACK),
                                       inv_sum[:], size_ps[:].rearrange("p j c -> p c j"), ALU.mult, ALU.mult)
        wg = turn(w, "a1", "w_grouped")
        g2 = turn(picked2, "a0", "v_grouped2")
        picked3 = gather_vector(3, "p_sum")
        g3 = turn(picked3, "x", "v_grouped3")

        v_codes = sbuf("v_codes", [P, E], U32)
        v_scales = sbuf("v_scales", [P, E], U8, tag="E")

        def quant_vals(j, grouped):
            nc.vector.quantize_mx(out=v_codes[:, j * P : (j + 1) * P].bitcast(FP8X4), scales=v_scales[:, j * P : (j + 1) * P],
                                  in_=grouped[:].rearrange("p r t -> p (r t)"))

        def product(tag, spans, copy):
            lo, hi = spans[0][0], spans[-1][1]
            o_ps = bank(tag, [P, hi - lo])
            for c0, c1 in spans:
                nc.tensor.matmul_mx(out=o_ps[:, c0 - lo : c1 - lo], lhsT=w_codes[:].bitcast(FP8X4), lhsT_scale=w_scales[:],
                                    rhs=v_codes[:, c0:c1].bitcast(FP8X4), rhs_scale=v_scales[:, c0:c1], start=True, stop=True)
            o_sb = sbuf("o_" + tag, [P, hi - lo], F32)
            copy(o_sb[:], o_ps[:])
            nc.sync.dma_start(out[:, lo:hi], o_sb[:])

        quant_vals(0, g0)
        quant_vals(1, g1)
        w_codes = sbuf("w_codes", [P, Q], U32)
        w_scales = sbuf("w_scales", [P, Q], U8)
        nc.vector.quantize_mx(out=w_codes[:].bitcast(FP8X4), scales=w_scales[:], in_=wg[:].rearrange("p r t -> p (r t)"))
        quant_vals(2, g2)
        product("bc2", [(0, 256), (256, 384)], nc.scalar.copy)
        quant_vals(3, g3)
        product("bc1", [(384, 512)], nc.vector.tensor_copy)
